import numpy as np
import ml_dtypes


def mxq(x, axis, fmt="e4m3"):
    dtype, down = {"e4m3": (ml_dtypes.float8_e4m3fn, 7), "e5m2": (ml_dtypes.float8_e5m2, 14)}[fmt]
    v = np.moveaxis(np.asarray(x, np.float32).astype(ml_dtypes.bfloat16).astype(np.float64), axis, -1)
    blocks = v.reshape(v.shape[:-1] + (-1, 32))
    amax = np.abs(blocks).max(-1, keepdims=True)
    byte = np.maximum(np.where(amax > 0, np.frexp(amax)[1] - 1 + 127, 0) - down, 1)
    scale = np.exp2(byte - 127.0)
    codes = (blocks / scale).astype(np.float32).astype(dtype).astype(np.float64)
    return np.moveaxis((codes * scale).reshape(v.shape), -1, axis)


WIDE = False


def mx_kscale(k):
    if not WIDE:
        return np.ones(k)
    levels = np.array([10, -10, 5, -5, 0])
    if k % 512:
        return np.exp2(np.random.permutation(np.resize(levels, k // 32))).repeat(32)
    a = np.empty((k // 512, 16))
    for p in range(k // 512):
        a[p, :8] = np.random.permutation(np.resize(levels, 8))
        for g in range(8):
            far = levels[np.abs(levels - a[p, g]) >= 10]
            a[p, g + 8] = far[np.random.randint(len(far))]
    return np.exp2(a.ravel()).repeat(32)


def f64(x):
    return np.asarray(x).astype(np.float64)


def striped8(idx):
    return np.concatenate([v.reshape(-1, 16).T for v in idx]).astype(np.uint16)


def unstriped8(offs):
    return np.stack([offs[16 * g:16 * g + 16].T.reshape(-1) for g in range(8)]).astype(np.int64)


def silu(v):
    return v / (1.0 + np.exp(-np.maximum(v, -700.0)))


K, M, T, S = 1024, 256, 1024, 512


def setup_inputs():
    n = np.random.standard_normal
    s = mx_kscale(K)[:, None]
    return {
        "x": (n((K, S)) * s).astype(np.float32),
        "w": (n((K, M)) / np.sqrt(K) / s).astype(np.float32),
        "b": (0.3 * n(256)).astype(np.float32),
        "wgo": np.repeat(np.random.uniform(0.5, 2.0, (8, S)), 16, axis=0).astype(np.float32),
        "offs": striped8(np.stack([np.random.permutation(T)[:S] for _ in range(8)])),
    }


def reference(x, w, b, wgo, offs):
    x_ = mxq(f64(x), 0, "e4m3")
    w_ = mxq(f64(w), 0, "e4m3")
    y = w_.T @ x_
    place = unstriped8(offs)[np.arange(M) % 128 // 16]
    out = np.zeros((M, T))
    out[np.arange(M)[:, None], place] = f64(wgo)[np.arange(M) % 128] * (silu(y + f64(b)[:, None]))
    return out

@@ -1,0 +1,120 @@
+from contextlib import ExitStack
+
+import concourse.mybir as mybir
+
+K, M, T, S = 1024, 256, 1024, 512
+FLOPS = 2 * K * M * S
+
+F32 = mybir.dt.float32
+BF16 = mybir.dt.bfloat16
+U32 = mybir.dt.uint32
+U16 = mybir.dt.uint16
+U8 = mybir.dt.uint8
+FP8X4 = mybir.dt.float8_e4m3fn_x4
+
+P = 128
+PACK = 4
+K_PASS = P * PACK
+PASSES = K // K_PASS
+HALF = S // 2
+M_TILES = M // P
+
+SILU = mybir.ActivationFunctionType.Silu
+MULT = mybir.AluOpType.mult
+
+
+def tile_list_hscat_silu_kernel(tc, x, w, b, wgo, offs, out):
+    nc = tc.nc
+    with ExitStack() as ctx:
+        keep = ctx.enter_context(tc.tile_pool(name="keep", bufs=1))
+        psum = ctx.enter_context(tc.psum_pool(name="psum", bufs=1))
+
+        offsets = keep.tile([P, S // 16], U16, name="offsets")
+        weights = keep.tile([P, S], F32, name="weights")
+        bias = keep.tile([P, M_TILES], F32, name="bias")
+        warm = keep.tile([P, 1], F32, name="warm")
+        windows = [keep.tile([P, T], F32, name=f"window{m}") for m in range(M_TILES)]
+        w_raw = [keep.tile([P, PACK, M], F32, name=f"w_raw{a}") for a in range(PASSES)]
+        x_raw = [[keep.tile([P, PACK, HALF], F32, name=f"x_raw{h}{a}") for a in range(PASSES)] for h in range(2)]
+
+        def operand(name, width):
+            grouped = keep.tile([P, width, PACK], BF16, align_bytes=64, name=f"grouped_{name}")
+            codes = keep.tile([P, width], U32, align_bytes=64, name=f"codes_{name}")
+            scales = keep.tile([P, width], U8, align_bytes=64, name=f"scales_{name}")
+            return grouped, codes, scales
+
+        w_mx = [operand(f"w{a}", M) for a in range(PASSES)]
+        x_mx = [[operand(f"x{h}{a}", HALF) for a in range(PASSES)] for h in range(2)]
+
+        w_view = w.rearrange("(a p j) n -> a p j n", p=P, j=PACK)
+        x_view = x.rearrange("(a p j) s -> a p j s", p=P, j=PACK)
+        with nc.allow_non_contiguous_dma(reason="one bias value a partition"):
+            nc.scalar.dma_start(out=bias[:], in_=b.rearrange("(m p) -> p m", p=P))
+        for a in range(PASSES):
+            nc.sync.dma_start(out=w_raw[a][:], in_=w_view[a])
+            nc.sync.dma_start(out=x_raw[0][a][:], in_=x_view[a][:, :, 0:HALF])
+        nc.sync.dma_start(out=offsets[:], in_=offs)
+        nc.sync.dma_start(out=weights[:], in_=wgo)
+        for a in range(PASSES):
+            nc.sync.dma_start(out=x_raw[1][a][:], in_=x_view[a][:, :, HALF:S])
+
+        nc.vector.memset(warm[:], 0.0)
+        nc.scalar.activation(out=warm[:], in_=warm[:], func=SILU)
+        for window in windows:
+            nc.vector.memset(window[:], 0.0)
+
+        def interleave(engine_copy, raw, grouped, lo, hi):
+            engine_copy(
+                out=grouped[:, lo:hi, :].rearrange("p (c i) t -> p c t i", i=4),
+                in_=raw[:, :, lo:hi].rearrange("p t (c i) -> p c t i", i=4),
+            )
+
+        def quantize(mx):
+            grouped, codes, scales = mx
+            nc.vector.quantize_mx(out=codes[:].bitcast(FP8X4), scales=scales[:], in_=grouped[:].rearrange("p c t -> p (c t)"))
+
+        def multiply(m, h):
+            acc = psum.tile([P, HALF], F32, name=f"acc{m}{h}")
+            cols = slice(m * P, (m + 1) * P)
+            for a in range(PASSES):
+                nc.tensor.matmul_mx(
+                    out=acc[:],
+                    lhsT=w_mx[a][1][:, cols].bitcast(FP8X4),
+                    lhsT_scale=w_mx[a][2][:, cols],
+                    rhs=x_mx[h][a][1][:].bitcast(FP8X4),
+                    rhs_scale=x_mx[h][a][2][:],
+                    start=(a == 0),
+                    stop=(a == PASSES - 1),
+                )
+            act = keep.tile([P, HALF], F32, name=f"act{m}{h}")
+            nc.scalar.activation(out=act[:], in_=acc[:], func=SILU, bias=bias[:, m : m + 1], scale=1.0)
+            return act
+
+        def scatter(m, h, act):
+            cols = slice(h * HALF, (h + 1) * HALF)
+            offs_cols = slice(h * HALF // 16, (h + 1) * HALF // 16)
+            nc.vector.tensor_tensor(
+                out=windows[m][:].indirect(offsets[:, offs_cols]), in0=act[:], in1=weights[:, cols], op=MULT
+            )
+
+        split = 160
+        for a in range(PASSES):
+            for raw, mx in ((w_raw[a], w_mx[a]), (x_raw[0][a], x_mx[0][a])):
+                interleave(nc.vector.tensor_copy, raw, mx[0], 0, split)
+                interleave(nc.scalar.copy, raw, mx[0], split, 256)
+                quantize(mx)
+        act00 = multiply(0, 0)
+        act10 = multiply(1, 0)
+        scatter(0, 0, act00)
+        interleave(nc.scalar.copy, x_raw[1][0], x_mx[1][0][0], 0, 256)
+        quantize(x_mx[1][0])
+        interleave(nc.vector.tensor_copy, x_raw[1][1], x_mx[1][1][0], 0, split)
+        interleave(nc.scalar.copy, x_raw[1][1], x_mx[1][1][0], split, 256)
+        quantize(x_mx[1][1])
+        act01 = multiply(0, 1)
+        act11 = multiply(1, 1)
+        scatter(1, 0, act10)
+        scatter(0, 1, act01)
+        nc.sync.dma_start(out=out[0:P, :], in_=windows[0][:])
+        scatter(1, 1, act11)
+        nc.sync.dma_start(out=out[P:M, :], in_=windows[1][:])

@@ -1,6 +1,7 @@
 from contextlib import ExitStack
 
 import concourse.mybir as mybir
+from concourse.masks import make_identity
 
 K, M, T, S = 1024, 256, 1024, 512
 FLOPS = 2 * K * M * S
@@ -30,12 +31,14 @@ def tile_list_hscat_silu_kernel(tc, x, w, b, wgo, offs, out):
         psum = ctx.enter_context(tc.psum_pool(name="psum", bufs=1))
 
         offsets = keep.tile([P, S // 16], U16, name="offsets")
-        weights = keep.tile([P, S], F32, name="weights")
+        weights = [keep.tile([P, HALF], F32, name=f"weights{h}") for h in range(2)]
+        bias_rows = keep.tile([P, P], F32, name="bias_rows")
+        identity = keep.tile([P, P], F32, name="identity")
         bias = keep.tile([P, M_TILES], F32, name="bias")
         warm = keep.tile([P, 1], F32, name="warm")
         windows = [keep.tile([P, T], F32, name=f"window{m}") for m in range(M_TILES)]
         w_raw = [keep.tile([P, PACK, M], F32, name=f"w_raw{a}") for a in range(PASSES)]
-        x_raw = [[keep.tile([P, PACK, HALF], F32, name=f"x_raw{h}{a}") for a in range(PASSES)] for h in range(2)]
+        x_raw = [[keep.tile([P, PACK, HALF], F32, name=f"x_raw{a}{h}", tag=f"slot{a}{h}") for h in range(2)] for a in range(PASSES)]
 
         def operand(name, width):
             grouped = keep.tile([P, width, PACK], BF16, align_bytes=64, name=f"grouped_{name}")
@@ -44,24 +47,35 @@ def tile_list_hscat_silu_kernel(tc, x, w, b, wgo, offs, out):
             return grouped, codes, scales
 
         w_mx = [operand(f"w{a}", M) for a in range(PASSES)]
-        x_mx = [[operand(f"x{h}{a}", HALF) for a in range(PASSES)] for h in range(2)]
+        x_mx = [[operand(f"x{a}{h}", HALF) for h in range(2)] for a in range(PASSES)]
 
         w_view = w.rearrange("(a p j) n -> a p j n", p=P, j=PACK)
         x_view = x.rearrange("(a p j) s -> a p j s", p=P, j=PACK)
-        with nc.allow_non_contiguous_dma(reason="one bias value a partition"):
-            nc.scalar.dma_start(out=bias[:], in_=b.rearrange("(m p) -> p m", p=P))
+
+        def load_x(a, h):
+            nc.sync.dma_start(out=x_raw[a][h][:], in_=x_view[a][:, :, h * HALF : (h + 1) * HALF])
+
+        def load_weights(h):
+            nc.sync.dma_start(out=weights[h][:], in_=wgo[:, h * HALF : (h + 1) * HALF])
+
+        nc.vector.memset(bias_rows[:], 0.0)
+        nc.scalar.dma_start(out=bias_rows[0:M_TILES, :], in_=b.rearrange("(m p) -> m p", p=P))
         for a in range(PASSES):
             nc.sync.dma_start(out=w_raw[a][:], in_=w_view[a])
-            nc.sync.dma_start(out=x_raw[0][a][:], in_=x_view[a][:, :, 0:HALF])
+            load_x(a, 0)
         nc.sync.dma_start(out=offsets[:], in_=offs)
-        nc.sync.dma_start(out=weights[:], in_=wgo)
-        for a in range(PASSES):
-            nc.sync.dma_start(out=x_raw[1][a][:], in_=x_view[a][:, :, HALF:S])
+        load_weights(0)
+        load_x(0, 1)
+        load_x(1, 1)
+        load_weights(1)
 
         nc.vector.memset(warm[:], 0.0)
         nc.scalar.activation(out=warm[:], in_=warm[:], func=SILU)
         for window in windows:
             nc.vector.memset(window[:], 0.0)
+        make_identity(nc, identity[:])
+        bias_bank = psum.tile([P, P], F32, name="bias_bank")
+        nc.tensor.transpose(bias_bank[:], bias_rows[:], identity[:])
 
         def interleave(engine_copy, raw, grouped, lo, hi):
             engine_copy(
@@ -73,46 +87,63 @@ def tile_list_hscat_silu_kernel(tc, x, w, b, wgo, offs, out):
             grouped, codes, scales = mx
             nc.vector.quantize_mx(out=codes[:].bitcast(FP8X4), scales=scales[:], in_=grouped[:].rearrange("p c t -> p (c t)"))
 
-        def multiply(m, h):
-            acc = psum.tile([P, HALF], F32, name=f"acc{m}{h}")
+        accs = {}
+
+        def multiply(m, h, a):
+            if a == 0:
+                accs[m, h] = psum.tile([P, HALF], F32, name=f"acc{m}{h}")
             cols = slice(m * P, (m + 1) * P)
-            for a in range(PASSES):
-                nc.tensor.matmul_mx(
-                    out=acc[:],
-                    lhsT=w_mx[a][1][:, cols].bitcast(FP8X4),
-                    lhsT_scale=w_mx[a][2][:, cols],
-                    rhs=x_mx[h][a][1][:].bitcast(FP8X4),
-                    rhs_scale=x_mx[h][a][2][:],
-                    start=(a == 0),
-                    stop=(a == PASSES - 1),
-                )
-            act = keep.tile([P, HALF], F32, name=f"act{m}{h}")
-            nc.scalar.activation(out=act[:], in_=acc[:], func=SILU, bias=bias[:, m : m + 1], scale=1.0)
+            nc.tensor.matmul_mx(
+                out=accs[m, h][:],
+                lhsT=w_mx[a][1][:, cols].bitcast(FP8X4),
+                lhsT_scale=w_mx[a][2][:, cols],
+                rhs=x_mx[a][h][1][:].bitcast(FP8X4),
+                rhs_scale=x_mx[a][h][2][:],
+                start=(a == 0),
+                stop=(a == PASSES - 1),
+            )
+
+        def activate(m, h):
+            act = keep.tile([P, HALF], F32, name=f"act{m}{h}", tag="slot11" if (m, h) == (1, 0) else f"act{m}{h}")
+            nc.scalar.activation(out=act[:], in_=accs[m, h][:], func=SILU, bias=bias[:, m : m + 1], scale=1.0)
             return act
 
         def scatter(m, h, act):
-            cols = slice(h * HALF, (h + 1) * HALF)
             offs_cols = slice(h * HALF // 16, (h + 1) * HALF // 16)
             nc.vector.tensor_tensor(
-                out=windows[m][:].indirect(offsets[:, offs_cols]), in0=act[:], in1=weights[:, cols], op=MULT
+                out=windows[m][:].indirect(offsets[:, offs_cols]), in0=act[:], in1=weights[h][:], op=MULT
             )
 
-        split = 160
-        for a in range(PASSES):
-            for raw, mx in ((w_raw[a], w_mx[a]), (x_raw[0][a], x_mx[0][a])):
-                interleave(nc.vector.tensor_copy, raw, mx[0], 0, split)
-                interleave(nc.scalar.copy, raw, mx[0], split, 256)
-                quantize(mx)
-        act00 = multiply(0, 0)
-        act10 = multiply(1, 0)
-        scatter(0, 0, act00)
-        interleave(nc.scalar.copy, x_raw[1][0], x_mx[1][0][0], 0, 256)
+        def share(raw, mx, split):
+            interleave(nc.vector.tensor_copy, raw, mx[0], 0, split)
+            interleave(nc.scalar.copy, raw, mx[0], split, 256)
+
+        interleave(nc.scalar.copy, w_raw[0], w_mx[0][0], 0, M)
+        share(x_raw[0][0], x_mx[0][0], 160)
+        quantize(w_mx[0])
+        quantize(x_mx[0][0])
+        multiply(0, 0, 0)
+        multiply(1, 0, 0)
+        share(w_raw[1], w_mx[1], 128)
+        quantize(w_mx[1])
+        nc.scalar.copy(out=bias[:], in_=bias_bank[:, 0:M_TILES])
+        share(x_raw[1][0], x_mx[1][0], 160)
         quantize(x_mx[1][0])
-        interleave(nc.vector.tensor_copy, x_raw[1][1], x_mx[1][1][0], 0, split)
-        interleave(nc.scalar.copy, x_raw[1][1], x_mx[1][1][0], split, 256)
+        multiply(0, 0, 1)
+        act00 = activate(0, 0)
+        multiply(1, 0, 1)
+        interleave(nc.vector.tensor_copy, x_raw[0][1], x_mx[0][1][0], 0, HALF)
+        scatter(0, 0, act00)
+        quantize(x_mx[0][1])
+        multiply(0, 1, 0)
+        multiply(1, 1, 0)
+        interleave(nc.scalar.copy, x_raw[1][1], x_mx[1][1][0], 0, HALF)
         quantize(x_mx[1][1])
-        act01 = multiply(0, 1)
-        act11 = multiply(1, 1)
+        act10 = activate(1, 0)
+        multiply(0, 1, 1)
+        act01 = activate(0, 1)
+        multiply(1, 1, 1)
+        act11 = activate(1, 1)
         scatter(1, 0, act10)
         scatter(0, 1, act01)
         nc.sync.dma_start(out=out[0:P, :], in_=windows[0][:])

@@ -83,30 +83,31 @@ def tile_list_hscat_silu_kernel(tc, x, w, b, wgo, offs, out):
                 in_=raw[:, :, lo:hi].rearrange("p t (c i) -> p c t i", i=4),
             )
 
-        def quantize(mx):
+        def quantize(mx, lo=0, hi=HALF):
             grouped, codes, scales = mx
-            nc.vector.quantize_mx(out=codes[:].bitcast(FP8X4), scales=scales[:], in_=grouped[:].rearrange("p c t -> p (c t)"))
+            nc.vector.quantize_mx(
+                out=codes[:, lo:hi].bitcast(FP8X4),
+                scales=scales[:, lo:hi],
+                in_=grouped[:, lo:hi, :].rearrange("p c t -> p (c t)"),
+            )
 
-        accs = {}
+        def bank(m, h, lo, hi):
+            return psum.tile([P, hi - lo], F32, name=f"acc{m}{h}_{lo}")
 
-        def multiply(m, h, a):
-            if a == 0:
-                accs[m, h] = psum.tile([P, HALF], F32, name=f"acc{m}{h}")
+        def multiply(acc, m, h, a, lo=0, hi=HALF):
             cols = slice(m * P, (m + 1) * P)
             nc.tensor.matmul_mx(
-                out=accs[m, h][:],
+                out=acc[:],
                 lhsT=w_mx[a][1][:, cols].bitcast(FP8X4),
                 lhsT_scale=w_mx[a][2][:, cols],
-                rhs=x_mx[a][h][1][:].bitcast(FP8X4),
-                rhs_scale=x_mx[a][h][2][:],
+                rhs=x_mx[a][h][1][:, lo:hi].bitcast(FP8X4),
+                rhs_scale=x_mx[a][h][2][:, lo:hi],
                 start=(a == 0),
                 stop=(a == PASSES - 1),
             )
 
-        def activate(m, h):
-            act = keep.tile([P, HALF], F32, name=f"act{m}{h}", tag="slot11" if (m, h) == (1, 0) else f"act{m}{h}")
-            nc.scalar.activation(out=act[:], in_=accs[m, h][:], func=SILU, bias=bias[:, m : m + 1], scale=1.0)
-            return act
+        def activate(act, acc, m, lo=0, hi=HALF):
+            nc.scalar.activation(out=act[:, lo:hi], in_=acc[:], func=SILU, bias=bias[:, m : m + 1], scale=1.0)
 
         def scatter(m, h, act):
             offs_cols = slice(h * HALF // 16, (h + 1) * HALF // 16)
@@ -118,32 +119,44 @@ def tile_list_hscat_silu_kernel(tc, x, w, b, wgo, offs, out):
             interleave(nc.vector.tensor_copy, raw, mx[0], 0, split)
             interleave(nc.scalar.copy, raw, mx[0], split, 256)
 
+        act00 = keep.tile([P, HALF], F32, name="act00")
+        pieces = [(0, 128), (128, 256)]
+        first_banks = [bank(0, 0, lo, hi) for lo, hi in pieces]
+        acc10 = bank(1, 0, 0, HALF)
+
         interleave(nc.scalar.copy, w_raw[0], w_mx[0][0], 0, M)
         share(x_raw[0][0], x_mx[0][0], 160)
         quantize(w_mx[0])
         quantize(x_mx[0][0])
-        multiply(0, 0, 0)
-        multiply(1, 0, 0)
+        for acc, (lo, hi) in zip(first_banks, pieces):
+            multiply(acc, 0, 0, 0, lo, hi)
+        multiply(acc10, 1, 0, 0)
         share(w_raw[1], w_mx[1], 128)
         quantize(w_mx[1])
         nc.scalar.copy(out=bias[:], in_=bias_bank[:, 0:M_TILES])
-        share(x_raw[1][0], x_mx[1][0], 160)
-        quantize(x_mx[1][0])
-        multiply(0, 0, 1)
-        act00 = activate(0, 0)
-        multiply(1, 0, 1)
+        share(x_raw[1][0], x_mx[1][0], 128)
+        for acc, (lo, hi) in zip(first_banks, pieces):
+            quantize(x_mx[1][0], lo, hi)
+            multiply(acc, 0, 0, 1, lo, hi)
+            activate(act00, acc, 0, lo, hi)
+        multiply(acc10, 1, 0, 1)
         interleave(nc.vector.tensor_copy, x_raw[0][1], x_mx[0][1][0], 0, HALF)
         scatter(0, 0, act00)
-        quantize(x_mx[0][1])
-        multiply(0, 1, 0)
-        multiply(1, 1, 0)
         interleave(nc.scalar.copy, x_raw[1][1], x_mx[1][1][0], 0, HALF)
+        quantize(x_mx[0][1])
+        acc01 = bank(0, 1, 0, HALF)
+        acc11 = bank(1, 1, 0, HALF)
+        multiply(acc01, 0, 1, 0)
+        multiply(acc11, 1, 1, 0)
         quantize(x_mx[1][1])
-        act10 = activate(1, 0)
-        multiply(0, 1, 1)
-        act01 = activate(0, 1)
-        multiply(1, 1, 1)
-        act11 = activate(1, 1)
+        act10 = keep.tile([P, HALF], F32, name="act10", tag="slot11")
+        activate(act10, acc10, 1)
+        act01 = keep.tile([P, HALF], F32, name="act01")
+        act11 = keep.tile([P, HALF], F32, name="act11")
+        multiply(acc01, 0, 1, 1)
+        activate(act01, acc01, 0)
+        multiply(acc11, 1, 1, 1)
+        activate(act11, acc11, 1)
         scatter(1, 0, act10)
         scatter(0, 1, act01)
         nc.sync.dma_start(out=out[0:P, :], in_=windows[0][:])

@@ -38,16 +38,22 @@ def tile_list_hscat_silu_kernel(tc, x, w, b, wgo, offs, out):
         warm = keep.tile([P, 1], F32, name="warm")
         windows = [keep.tile([P, T], F32, name=f"window{m}") for m in range(M_TILES)]
         w_raw = [keep.tile([P, PACK, M], F32, name=f"w_raw{a}") for a in range(PASSES)]
-        x_raw = [[keep.tile([P, PACK, HALF], F32, name=f"x_raw{a}{h}", tag=f"slot{a}{h}") for h in range(2)] for a in range(PASSES)]
+        x0_raw = keep.tile([P, PACK, S], F32, name="x0_raw")
+        x_raw = [
+            [x0_raw[:, :, 0:HALF], x0_raw[:, :, HALF:S]],
+            [keep.tile([P, PACK, HALF], F32, name=f"x1_raw{h}", tag=f"slot1{h}") for h in range(2)],
+        ]
+
+        first_bias = keep.tile([P, M_TILES], F32, align_bytes=64, name="first_bias", tag="late")
 
         def operand(name, width):
-            grouped = keep.tile([P, width, PACK], BF16, align_bytes=64, name=f"grouped_{name}")
+            grouped = keep.tile([P, width, PACK], BF16, align_bytes=64, name=f"grouped_{name}", tag="late" if name == "x11" else f"grouped_{name}")
             codes = keep.tile([P, width], U32, align_bytes=64, name=f"codes_{name}")
             scales = keep.tile([P, width], U8, align_bytes=64, name=f"scales_{name}")
             return grouped, codes, scales
 
         w_mx = [operand(f"w{a}", M) for a in range(PASSES)]
-        x_mx = [[operand(f"x{a}{h}", HALF) for h in range(2)] for a in range(PASSES)]
+        x_mx = [[operand("x00", HALF), operand("x01", HALF)], [operand("x10", HALF)]]
 
         w_view = w.rearrange("(a p j) n -> a p j n", p=P, j=PACK)
         x_view = x.rearrange("(a p j) s -> a p j s", p=P, j=PACK)
@@ -60,12 +66,12 @@ def tile_list_hscat_silu_kernel(tc, x, w, b, wgo, offs, out):
 
         nc.vector.memset(bias_rows[:], 0.0)
         nc.scalar.dma_start(out=bias_rows[0:M_TILES, :], in_=b.rearrange("(m p) -> m p", p=P))
-        for a in range(PASSES):
-            nc.sync.dma_start(out=w_raw[a][:], in_=w_view[a])
-            load_x(a, 0)
+        nc.sync.dma_start(out=w_raw[0][:], in_=w_view[0])
+        nc.sync.dma_start(out=x0_raw[:], in_=x_view[0])
+        load_x(1, 0)
+        nc.sync.dma_start(out=w_raw[1][:], in_=w_view[1])
         nc.sync.dma_start(out=offsets[:], in_=offs)
         load_weights(0)
-        load_x(0, 1)
         load_x(1, 1)
         load_weights(1)
 
@@ -106,7 +112,7 @@ def tile_list_hscat_silu_kernel(tc, x, w, b, wgo, offs, out):
                 stop=(a == PASSES - 1),
             )
 
-        def activate(act, acc, m, lo=0, hi=HALF):
+        def activate(act, acc, m, bias, lo=0, hi=HALF):
             nc.scalar.activation(out=act[:, lo:hi], in_=acc[:], func=SILU, bias=bias[:, m : m + 1], scale=1.0)
 
         def scatter(m, h, act):
@@ -127,36 +133,41 @@ def tile_list_hscat_silu_kernel(tc, x, w, b, wgo, offs, out):
         interleave(nc.scalar.copy, w_raw[0], w_mx[0][0], 0, M)
         share(x_raw[0][0], x_mx[0][0], 160)
         quantize(w_mx[0])
+        share(x_raw[0][1], x_mx[0][1], 128)
         quantize(x_mx[0][0])
+        quantize(x_mx[0][1])
         for acc, (lo, hi) in zip(first_banks, pieces):
             multiply(acc, 0, 0, 0, lo, hi)
         multiply(acc10, 1, 0, 0)
-        share(w_raw[1], w_mx[1], 128)
-        quantize(w_mx[1])
+        share(x_raw[1][0], x_mx[1][0], 160)
+        quantize(x_mx[1][0])
+        nc.scalar.copy(out=first_bias[:], in_=bias_bank[:, 0:M_TILES])
         nc.scalar.copy(out=bias[:], in_=bias_bank[:, 0:M_TILES])
-        share(x_raw[1][0], x_mx[1][0], 128)
+        interleave(nc.vector.tensor_copy, w_raw[1], w_mx[1][0], 0, 64)
+        interleave(nc.scalar.copy, w_raw[1], w_mx[1][0], 64, 128)
+        interleave(nc.scalar.copy, w_raw[1], w_mx[1][0], 128, 256)
+        quantize(w_mx[1], 0, 128)
         for acc, (lo, hi) in zip(first_banks, pieces):
-            quantize(x_mx[1][0], lo, hi)
             multiply(acc, 0, 0, 1, lo, hi)
-            activate(act00, acc, 0, lo, hi)
+            activate(act00, acc, 0, first_bias, lo, hi)
+        quantize(w_mx[1], 128, 256)
         multiply(acc10, 1, 0, 1)
-        interleave(nc.vector.tensor_copy, x_raw[0][1], x_mx[0][1][0], 0, HALF)
         scatter(0, 0, act00)
+        x_mx[1].append(operand("x11", HALF))
         interleave(nc.scalar.copy, x_raw[1][1], x_mx[1][1][0], 0, HALF)
-        quantize(x_mx[0][1])
         acc01 = bank(0, 1, 0, HALF)
         acc11 = bank(1, 1, 0, HALF)
         multiply(acc01, 0, 1, 0)
         multiply(acc11, 1, 1, 0)
         quantize(x_mx[1][1])
         act10 = keep.tile([P, HALF], F32, name="act10", tag="slot11")
-        activate(act10, acc10, 1)
+        activate(act10, acc10, 1, bias)
         act01 = keep.tile([P, HALF], F32, name="act01")
         act11 = keep.tile([P, HALF], F32, name="act11")
         multiply(acc01, 0, 1, 1)
-        activate(act01, acc01, 0)
+        activate(act01, acc01, 0, bias)
         multiply(acc11, 1, 1, 1)
-        activate(act11, acc11, 1)
+        activate(act11, acc11, 1, bias)
         scatter(1, 0, act10)
         scatter(0, 1, act01)
         nc.sync.dma_start(out=out[0:P, :], in_=windows[0][:])

from contextlib import ExitStack

import concourse.mybir as mybir
from concourse.masks import make_identity

K, M, T, S = 1024, 256, 1024, 512
FLOPS = 2 * K * M * S

F32 = mybir.dt.float32
BF16 = mybir.dt.bfloat16
U32 = mybir.dt.uint32
U16 = mybir.dt.uint16
U8 = mybir.dt.uint8
FP8X4 = mybir.dt.float8_e4m3fn_x4

P = 128
PACK = 4
K_PASS = P * PACK
PASSES = K // K_PASS
HALF = S // 2
M_TILES = M // P

SILU = mybir.ActivationFunctionType.Silu
MULT = mybir.AluOpType.mult


def tile_list_hscat_silu_kernel(tc, x, w, b, wgo, offs, out):
    nc = tc.nc
    with ExitStack() as ctx:
        keep = ctx.enter_context(tc.tile_pool(name="keep", bufs=1))
        psum = ctx.enter_context(tc.psum_pool(name="psum", bufs=1))

        offsets = keep.tile([P, S // 16], U16, name="offsets")
        weights = [keep.tile([P, HALF], F32, name=f"weights{h}") for h in range(2)]
        bias_rows = keep.tile([P, P], F32, name="bias_rows")
        identity = keep.tile([P, P], F32, name="identity")
        bias = keep.tile([P, M_TILES], F32, name="bias")
        warm = keep.tile([P, 1], F32, name="warm")
        windows = [keep.tile([P, T], F32, name=f"window{m}") for m in range(M_TILES)]
        w_raw = [keep.tile([P, PACK, M], F32, name=f"w_raw{a}") for a in range(PASSES)]
        x0_raw = keep.tile([P, PACK, S], F32, name="x0_raw")
        x_raw = [
            [x0_raw[:, :, 0:HALF], x0_raw[:, :, HALF:S]],
            [keep.tile([P, PACK, HALF], F32, name=f"x1_raw{h}", tag=f"slot1{h}") for h in range(2)],
        ]

        first_bias = keep.tile([P, M_TILES], F32, align_bytes=64, name="first_bias", tag="late")

        def operand(name, width):
            grouped = keep.tile([P, width, PACK], BF16, align_bytes=64, name=f"grouped_{name}", tag="late" if name == "x11" else f"grouped_{name}")
            codes = keep.tile([P, width], U32, align_bytes=64, name=f"codes_{name}")
            scales = keep.tile([P, width], U8, align_bytes=64, name=f"scales_{name}")
            return grouped, codes, scales

        w_mx = [operand(f"w{a}", M) for a in range(PASSES)]
        x_mx = [[operand("x00", HALF), operand("x01", HALF)], [operand("x10", HALF)]]

        w_view = w.rearrange("(a p j) n -> a p j n", p=P, j=PACK)
        x_view = x.rearrange("(a p j) s -> a p j s", p=P, j=PACK)

        def load_x(a, h):
            nc.sync.dma_start(out=x_raw[a][h][:], in_=x_view[a][:, :, h * HALF : (h + 1) * HALF])

        def load_weights(h):
            nc.sync.dma_start(out=weights[h][:], in_=wgo[:, h * HALF : (h + 1) * HALF])

        nc.vector.memset(bias_rows[:], 0.0)
        nc.scalar.dma_start(out=bias_rows[0:M_TILES, :], in_=b.rearrange("(m p) -> m p", p=P))
        nc.sync.dma_start(out=w_raw[0][:], in_=w_view[0])
        nc.sync.dma_start(out=x0_raw[:], in_=x_view[0])
        load_x(1, 0)
        nc.sync.dma_start(out=w_raw[1][:], in_=w_view[1])
        nc.sync.dma_start(out=offsets[:], in_=offs)
        load_weights(0)
        load_x(1, 1)
        load_weights(1)

        nc.vector.memset(warm[:], 0.0)
        nc.scalar.activation(out=warm[:], in_=warm[:], func=SILU)
        for window in windows:
            nc.vector.memset(window[:], 0.0)
        make_identity(nc, identity[:])
        bias_bank = psum.tile([P, P], F32, name="bias_bank")
        nc.tensor.transpose(bias_bank[:], bias_rows[:], identity[:])

        def interleave(engine_copy, raw, grouped, lo, hi):
            engine_copy(
                out=grouped[:, lo:hi, :].rearrange("p (c i) t -> p c t i", i=4),
                in_=raw[:, :, lo:hi].rearrange("p t (c i) -> p c t i", i=4),
            )

        def quantize(mx, lo=0, hi=HALF):
            grouped, codes, scales = mx
            nc.vector.quantize_mx(
                out=codes[:, lo:hi].bitcast(FP8X4),
                scales=scales[:, lo:hi],
                in_=grouped[:, lo:hi, :].rearrange("p c t -> p (c t)"),
            )

        def bank(m, h, lo, hi):
            return psum.tile([P, hi - lo], F32, name=f"acc{m}{h}_{lo}")

        def multiply(acc, m, h, a, lo=0, hi=HALF):
            cols = slice(m * P, (m + 1) * P)
            nc.tensor.matmul_mx(
                out=acc[:],
                lhsT=w_mx[a][1][:, cols].bitcast(FP8X4),
                lhsT_scale=w_mx[a][2][:, cols],
                rhs=x_mx[a][h][1][:, lo:hi].bitcast(FP8X4),
                rhs_scale=x_mx[a][h][2][:, lo:hi],
                start=(a == 0),
                stop=(a == PASSES - 1),
            )

        def activate(act, acc, m, bias, lo=0, hi=HALF):
            nc.scalar.activation(out=act[:, lo:hi], in_=acc[:], func=SILU, bias=bias[:, m : m + 1], scale=1.0)

        def scatter(m, h, act):
            offs_cols = slice(h * HALF // 16, (h + 1) * HALF // 16)
            nc.vector.tensor_tensor(
                out=windows[m][:].indirect(offsets[:, offs_cols]), in0=act[:], in1=weights[h][:], op=MULT
            )

        def share(raw, mx, split):
            interleave(nc.vector.tensor_copy, raw, mx[0], 0, split)
            interleave(nc.scalar.copy, raw, mx[0], split, 256)

        act00 = keep.tile([P, HALF], F32, name="act00")
        pieces = [(0, 128), (128, 256)]
        first_banks = [bank(0, 0, lo, hi) for lo, hi in pieces]
        acc10 = bank(1, 0, 0, HALF)

        interleave(nc.scalar.copy, w_raw[0], w_mx[0][0], 0, M)
        share(x_raw[0][0], x_mx[0][0], 160)
        quantize(w_mx[0])
        share(x_raw[0][1], x_mx[0][1], 128)
        quantize(x_mx[0][0])
        quantize(x_mx[0][1])
        for acc, (lo, hi) in zip(first_banks, pieces):
            multiply(acc, 0, 0, 0, lo, hi)
        multiply(acc10, 1, 0, 0)
        share(x_raw[1][0], x_mx[1][0], 160)
        quantize(x_mx[1][0])
        nc.scalar.copy(out=first_bias[:], in_=bias_bank[:, 0:M_TILES])
        nc.scalar.copy(out=bias[:], in_=bias_bank[:, 0:M_TILES])
        interleave(nc.vector.tensor_copy, w_raw[1], w_mx[1][0], 0, 64)
        interleave(nc.scalar.copy, w_raw[1], w_mx[1][0], 64, 128)
        interleave(nc.scalar.copy, w_raw[1], w_mx[1][0], 128, 256)
        quantize(w_mx[1], 0, 128)
        for acc, (lo, hi) in zip(first_banks, pieces):
            multiply(acc, 0, 0, 1, lo, hi)
            activate(act00, acc, 0, first_bias, lo, hi)
        quantize(w_mx[1], 128, 256)
        multiply(acc10, 1, 0, 1)
        scatter(0, 0, act00)
        x_mx[1].append(operand("x11", HALF))
        interleave(nc.scalar.copy, x_raw[1][1], x_mx[1][1][0], 0, HALF)
        acc01 = bank(0, 1, 0, HALF)
        acc11 = bank(1, 1, 0, HALF)
        multiply(acc01, 0, 1, 0)
        multiply(acc11, 1, 1, 0)
        quantize(x_mx[1][1])
        act10 = keep.tile([P, HALF], F32, name="act10", tag="slot11")
        activate(act10, acc10, 1, bias)
        act01 = keep.tile([P, HALF], F32, name="act01")
        act11 = keep.tile([P, HALF], F32, name="act11")
        multiply(acc01, 0, 1, 1)
        activate(act01, acc01, 0, bias)
        multiply(acc11, 1, 1, 1)
        activate(act11, acc11, 1, bias)
        scatter(1, 0, act10)
        scatter(0, 1, act01)
        nc.sync.dma_start(out=out[0:P, :], in_=windows[0][:])
        scatter(1, 1, act11)
        nc.sync.dma_start(out=out[P:M, :], in_=windows[1][:])
